import numpy as np
import ml_dtypes


def mxq(x, axis, fmt="e4m3"):
    dtype, down = {"e4m3": (ml_dtypes.float8_e4m3fn, 7), "e5m2": (ml_dtypes.float8_e5m2, 14)}[fmt]
    v = np.moveaxis(np.asarray(x, np.float32).astype(ml_dtypes.bfloat16).astype(np.float64), axis, -1)
    blocks = v.reshape(v.shape[:-1] + (-1, 32))
    amax = np.abs(blocks).max(-1, keepdims=True)
    byte = np.maximum(np.where(amax > 0, np.frexp(amax)[1] - 1 + 127, 0) - down, 1)
    scale = np.exp2(byte - 127.0)
    codes = (blocks / scale).astype(np.float32).astype(dtype).astype(np.float64)
    return np.moveaxis((codes * scale).reshape(v.shape), -1, axis)


WIDE = False


def mx_kscale(k):
    if not WIDE:
        return np.ones(k)
    levels = np.array([10, -10, 5, -5, 0])
    if k % 512:
        return np.exp2(np.random.permutation(np.resize(levels, k // 32))).repeat(32)
    a = np.empty((k // 512, 16))
    for p in range(k // 512):
        a[p, :8] = np.random.permutation(np.resize(levels, 8))
        for g in range(8):
            far = levels[np.abs(levels - a[p, g]) >= 10]
            a[p, g + 8] = far[np.random.randint(len(far))]
    return np.exp2(a.ravel()).repeat(32)


def f64(x):
    return np.asarray(x).astype(np.float64)


def striped(idx):
    return np.tile(idx.reshape(-1, 16).T, (8, 1)).astype(np.uint16)


def unstriped(offs):
    return offs[:16].T.reshape(-1).astype(np.int64)


def striped8(idx):
    return np.concatenate([x.reshape(-1, 16).T for x in idx]).astype(np.uint16)


def runs(offs, k):
    lists = np.stack([offs[16 * r : 16 * r + 16].T.reshape(-1) for r in range(8)]).astype(np.int64)
    return lists[np.arange(k) % 512 // 64]


def pack_weight(w):
    k, n = w.shape
    w = f64(np.asarray(w, np.float32).astype(ml_dtypes.bfloat16)).reshape(k // 32, 32, n)
    amax = np.abs(w).max(1)
    byte = np.clip(np.where(amax > 0, np.frexp(amax)[1] - 1 + 127 - 7, 1), 1, 254)
    scaled = (w * np.exp2(127.0 - byte)[:, None, :]).reshape(k, n).astype(np.float32)
    words = np.ascontiguousarray(scaled.reshape(k // 512, 128, 4, n).transpose(0, 1, 3, 2)).astype(ml_dtypes.float8_e4m3fn).view(np.uint8)
    return words, np.ascontiguousarray(byte.astype(np.uint8).reshape(k // 512, 16, n))


def unpack_weight(words, scales):
    g, p, n, _ = words.shape
    vals = np.ascontiguousarray(words).view(ml_dtypes.float8_e4m3fn).astype(np.float64) * np.repeat(np.exp2(scales.astype(np.float64) - 127.0), 8, axis=1)[..., None]
    return vals.transpose(0, 1, 3, 2).reshape(g * 512, n)


def sigmoid(v):
    return 1.0 / (1.0 + np.exp(-np.maximum(v, -700.0)))

def planes(y):
    n, m = y.shape
    v = y.astype(np.float32).astype(ml_dtypes.bfloat16).astype(np.float64).reshape(n // 32, 32, m)
    top = np.abs(v).max(1)
    byte = np.clip(np.where(top > 0, np.frexp(top)[1] - 1 + 127 - 7, 1), 1, 254)
    codes = (v * np.exp2(127.0 - byte)[:, None, :]).reshape(n, m).astype(np.float32).astype(ml_dtypes.float8_e4m3fn).view(np.uint8)
    words = codes.reshape(n // 512, 128, 4, m).transpose(0, 1, 3, 2)
    return np.ascontiguousarray(words), np.ascontiguousarray(byte.astype(np.uint8).reshape(n // 512, 16, m))


K, T, S, N, G, H = 512, 1024, 512, 512, 2048, 512


def setup_inputs():
    n = np.random.standard_normal
    s = mx_kscale(K)[:, None]
    u = mx_kscale(S)
    packed_xT = pack_weight(n((K, T)) * s)
    packed_dT = pack_weight(n((K, G)) / s)
    packed_w1 = pack_weight(n((H, N)) / np.sqrt(2 * H) / u[:, None])
    packed_w2 = pack_weight(n((K, N)) / np.sqrt(2 * K) / s)
    return {
        "x_words": packed_xT[0],
        "x_scales": packed_xT[1],
        "d_words": packed_dT[0],
        "d_scales": packed_dT[1],
        "sl": np.random.uniform(1.0, 2.0, (H, 1)).astype(np.float32),
        "th": (0.5 * n((H, 1))).astype(np.float32),
        "gn": (np.random.uniform(0.5, 1.5, (H, 1)) * u[:, None]).astype(np.float32),
        "w1_words": packed_w1[0],
        "w1_scales": packed_w1[1],
        "w2_words": packed_w2[0],
        "w2_scales": packed_w2[1],
        "tau": np.random.uniform(0.3, 0.9, (N, 1)).astype(np.float32),
        "offs": striped(np.random.permutation(T)[:S]),
        "k1": striped8(np.random.randint(0, G, (8, H))),
        "n1": striped(np.random.permutation(S)),
        "n2": striped(np.random.permutation(S)),
        "two": striped(np.random.permutation(T)[:S]),
        "n3": striped(np.random.permutation(S)),
        "n4": striped(np.random.permutation(S)),
    }


def reference(x_words, x_scales, d_words, d_scales, sl, th, gn, w1_words, w1_scales, w2_words, w2_scales, tau, offs, k1, n1, n2, two, n3, n4):
    d_k1 = unpack_weight(d_words, d_scales)[np.arange(K)[:, None], runs(k1, K)]
    xq = unpack_weight(x_words, x_scales)[:, unstriped(offs)]
    h = 0.0625 * (d_k1.T @ xq)
    sg = sigmoid(f64(sl) * (h[:, unstriped(n1)] - f64(th)))
    z = f64(gn) * (np.maximum(h * sg, 0.75 * h[:, unstriped(n2)]))
    x_two = unpack_weight(x_words, x_scales)[:, unstriped(two)]
    h2 = unpack_weight(w1_words, w1_scales).T @ mxq(z, 0, "e4m3") + unpack_weight(w2_words, w2_scales).T @ x_two
    top = h2.max(axis=1, keepdims=True)
    ea = np.exp(f64(tau) * (h2[:, unstriped(n4)] - top))
    out_0 = (0.5 * (h2 - h2[:, unstriped(n3)])) / (ea + 0.25)
    return (out_0,) + planes(out_0)

@@ -1,0 +1,246 @@
+from contextlib import ExitStack
+
+import concourse.mybir as mybir
+
+F32 = mybir.dt.float32
+BF16 = mybir.dt.bfloat16
+I32 = mybir.dt.int32
+U32 = mybir.dt.uint32
+U16 = mybir.dt.uint16
+U8 = mybir.dt.uint8
+FP8X4 = mybir.dt.float8_e4m3fn_x4
+ALU = mybir.AluOpType
+ACT = mybir.ActivationFunctionType
+
+P = 128
+PACK = 4
+T, S, G = 1024, 512, 2048
+FLOPS = 3 * 2 * 512 * 512 * 512
+
+Z_PIECES = ((0, 256), (256, 128), (384, 128))
+HALVES = ((0, 256), (256, 256))
+OUT_PIECES = ((0, 128), (128, 128), (256, 128), (384, 128))
+
+
+def words_of(dram):
+    return dram[0].rearrange("p n r -> p (n r)").bitcast(I32)
+
+
+def entries(offsets, start, width):
+    return offsets[:, start // 16 : (start + width) // 16]
+
+
+def deal(copy, dst, src):
+    copy(
+        out=dst.rearrange("p (t c i) -> p c t i", t=PACK, i=4),
+        in_=src.rearrange("p (c i t) -> p c t i", t=PACK, i=4),
+    )
+
+
+def tile_picked_pqmixemoera_none_po_kernel(
+    tc, x_words, x_scales, d_words, d_scales, sl, th, gn, w1_words, w1_scales, w2_words, w2_scales, tau,
+    offs, k1, n1, n2, two, n3, n4, out_0, out_1, out_2,
+):
+    nc = tc.nc
+    with ExitStack() as ctx:
+        lists = ctx.enter_context(tc.tile_pool(name="lists", bufs=1))
+        sb = ctx.enter_context(tc.tile_pool(name="sb", bufs=1))
+        shared = ctx.enter_context(tc.tile_pool(name="shared", bufs=1))
+        psum = ctx.enter_context(tc.psum_pool(name="psum", bufs=1))
+
+        def load_list(dram, name):
+            offsets = lists.tile([P, S // 16], U16, name=name)
+            nc.sync.dma_start(offsets[:], dram)
+            return offsets
+
+        def load_rows(dram, name):
+            column = sb.tile([P, PACK], F32, name=name)
+            nc.gpsimd.dma_start(column[:], dram.rearrange("(p t) o -> p (t o)", t=PACK))
+            return column
+
+        dk_plane = sb.tile([P, S], U8, name="dk_plane", align_bytes=64)
+        nc.gpsimd.memset(dk_plane[:].bitcast(I32), 0)
+
+        k1_sb = load_list(k1, "k1_sb")
+        d_bytes = sb.tile([P, G], U8, name="d_bytes")
+        nc.sync.dma_start(
+            d_bytes[:].bitcast(I32),
+            d_scales[0].bitcast(I32).unsqueeze(1).to_broadcast([16, 8, G // 4]),
+        )
+        offs_sb = load_list(offs, "offs_sb")
+        x_bytes = sb.tile([P, T], U8, name="x_bytes")
+        for q in range(4):
+            nc.sync.dma_start(
+                x_bytes[32 * q : 32 * q + 32, :].bitcast(I32),
+                x_scales[0, 4 * q : 4 * q + 4, :].bitcast(I32).unsqueeze(0).to_broadcast([8, 4, T // 4]),
+            )
+        d_table = shared.tile([P, G], I32, name="d_table", align_bytes=64, offset=4096)
+        nc.sync.dma_start(d_table[:], words_of(d_words))
+        n1_sb = load_list(n1, "n1_sb")
+        n2_sb = load_list(n2, "n2_sb")
+        two_sb = load_list(two, "two_sb")
+        n3_sb = load_list(n3, "n3_sb")
+        x_table = sb.tile([P, T], I32, name="x_table")
+        nc.sync.dma_start(x_table[:], words_of(x_words))
+        w2_raw = sb.tile([P, S], I32, name="w2_raw")
+        nc.sync.dma_start(w2_raw[:], words_of(w2_words))
+        w1_raw = sb.tile([P, S], I32, name="w1_raw")
+        nc.sync.dma_start(w1_raw[:], words_of(w1_words))
+        n4_sb = load_list(n4, "n4_sb")
+        sl_sb = load_rows(sl, "sl_sb")
+        th_sb = load_rows(th, "th_sb")
+        sl_th = sb.tile([P, PACK], F32, name="sl_th")
+        nc.gpsimd.tensor_tensor(sl_th[:], sl_sb[:], th_sb[:], ALU.mult)
+        sg_bias = sb.tile([P, PACK], F32, name="sg_bias")
+        nc.gpsimd.tensor_scalar(sg_bias[:], sl_th[:], -1.0, 1.0, ALU.mult, ALU.mult)
+        gn_sb = load_rows(gn, "gn_sb")
+        tau_sb = load_rows(tau, "tau_sb")
+
+        dk_bytes = sb.tile([P, S], U8, name="dk_bytes", tag="w1_codes", align_bytes=64)
+        nc.vector.tensor_copy(dk_bytes[:], d_bytes[:].indirect(k1_sb[:]))
+        dk_dealt = sb.tile([P, S], U8, name="dk_dealt", tag="w2_codes", align_bytes=64)
+        deal(nc.vector.tensor_copy, dk_dealt[:], dk_bytes[:])
+        for q in range(4):
+            nc.scalar.dma_start(
+                dk_plane[32 * q : 32 * q + 4, :].bitcast(I32),
+                dk_dealt[32 * q : 32 * q + 32 : 8, :].bitcast(I32),
+            )
+        xq_plane = sb.tile([P, S], U8, name="xq_plane", align_bytes=64)
+        nc.vector.tensor_copy(xq_plane[:], x_bytes[:].indirect(offs_sb[:]))
+        dk_words = sb.tile([P, S], U32, name="dk_words")
+        nc.vector.tensor_copy(dk_words[:], d_table[:].bitcast(U32).indirect(k1_sb[:]))
+        dk_codes = [shared.tile([P, P], I32, name="dk_codes0", align_bytes=64, offset=1792)]
+        dk_codes.extend(sb.tile([P, P], I32, name=f"dk_codes{t}", align_bytes=64) for t in range(1, PACK - 1))
+        dk_codes.append(sb.tile([P, P], I32, name="dk_codes3", tag="w_planes", align_bytes=64))
+        nc.vector.tensor_copy(dk_codes[0][:], dk_words[:].bitcast(I32)[:, 0::PACK])
+        xq_codes = shared.tile([P, S], U32, name="xq_codes", align_bytes=64, offset=4096)
+        for start, width in HALVES:
+            nc.vector.tensor_copy(
+                xq_codes[:, start : start + width], x_table[:].bitcast(U32).indirect(entries(offs_sb, start, width))
+            )
+
+        w2_codes = sb.tile([P, S], U32, name="w2_codes", tag="w2_codes", align_bytes=64)
+        deal(nc.scalar.copy, w2_codes[:], w2_raw[:].bitcast(U32))
+        w1_codes = sb.tile([P, S], U32, name="w1_codes", tag="w1_codes", align_bytes=64)
+        deal(nc.scalar.copy, w1_codes[:], w1_raw[:].bitcast(U32))
+
+        w_bytes = shared.tile([P, S], U8, name="w_bytes", align_bytes=64, offset=8192)
+        nc.gpsimd.memset(w_bytes[:].bitcast(I32), 0)
+        for place, scales in ((4, w2_scales), (0, w1_scales)):
+            for q in range(4):
+                nc.sync.dma_start(
+                    w_bytes[32 * q + place : 32 * q + place + 4, :].bitcast(I32),
+                    scales[0, 4 * q : 4 * q + 4, :].bitcast(I32),
+                )
+
+        h_rows = [sb.tile([P, S], F32, name=f"h_rows{t}") for t in range(PACK)]
+
+        def first_product(t, start, width, bank_name):
+            bank = psum.tile([P, S], F32, name=bank_name)
+            rows, cols = slice(P * t, P * (t + 1)), slice(start, start + width)
+            nc.tensor.matmul_mx(
+                out=bank[:, :width], lhsT=dk_codes[t][:].bitcast(FP8X4), lhsT_scale=dk_plane[:, rows],
+                rhs=xq_codes[:, cols].bitcast(FP8X4), rhs_scale=xq_plane[:, cols], start=True, stop=True,
+            )
+            return bank[:, :width]
+
+        for (start, width), bank_name in zip(HALVES, ("h_first", "h_bank")):
+            nc.vector.tensor_scalar(
+                h_rows[0][:, start : start + width], first_product(0, start, width, bank_name), 0.0625, None, ALU.mult
+            )
+        for t in range(1, PACK):
+            nc.vector.tensor_copy(dk_codes[t][:], dk_words[:].bitcast(I32)[:, t::PACK])
+
+        x2_codes = shared.tile([P, S], U32, name="x2_codes", align_bytes=64, offset=0)
+        nc.vector.tensor_copy(x2_codes[:], x_table[:].bitcast(U32).indirect(two_sb[:]))
+        x2_plane = shared.tile([P, S], U8, name="x2_plane", align_bytes=64, offset=2048)
+        nc.vector.tensor_copy(x2_plane[:], x_bytes[:].indirect(two_sb[:]))
+
+        h2_banks = [psum.tile([P, S], F32, name=f"h2_bank{t}") for t in range(PACK)]
+        h2_rows = [sb.tile([P, S], F32, name=f"h2_rows{t}") for t in range(PACK)]
+        for piece, (start, width) in enumerate(Z_PIECES):
+            cols = slice(start, start + width)
+            sg = sb.tile([P, PACK, width], F32, name=f"sg{piece}")
+            h_n2 = sb.tile([P, PACK, width], F32, name=f"h_n2{piece}")
+            gated = sb.tile([P, PACK, width], F32, name=f"gated{piece}")
+            larger = sb.tile([P, PACK, width], F32, name=f"larger{piece}")
+            for t in range(PACK):
+                if piece == 0 and t > 0:
+                    nc.scalar.activation(h_rows[t][:], first_product(t, 0, S, "h_bank"), ACT.Copy, scale=0.0625)
+                nc.scalar.activation(
+                    sg[:, t, :], h_rows[t][:].indirect(entries(n1_sb, start, width)), ACT.Sigmoid,
+                    bias=sg_bias[:, t : t + 1], scale=sl_sb[:, t : t + 1],
+                )
+                nc.scalar.activation(h_n2[:, t, :], h_rows[t][:].indirect(entries(n2_sb, start, width)), ACT.Copy)
+                nc.vector.tensor_tensor(gated[:, t, :], h_rows[t][:, cols], sg[:, t, :], ALU.mult)
+                nc.vector.scalar_tensor_tensor(larger[:, t, :], h_n2[:, t, :], 0.75, gated[:, t, :], ALU.mult, ALU.max)
+            if piece == 0:
+                w_planes = sb.tile([P, S], U8, name="w_planes", tag="w_planes", align_bytes=64)
+                deal(nc.vector.tensor_copy, w_planes[:], w_bytes[:])
+                for t in range(PACK):
+                    rows = slice(P * t, P * (t + 1))
+                    nc.tensor.matmul_mx(
+                        out=h2_banks[t][:], lhsT=w2_codes[:, rows].bitcast(FP8X4), lhsT_scale=w_planes[4:P, rows],
+                        rhs=x2_codes[:].bitcast(FP8X4), rhs_scale=x2_plane[:], start=True, stop=False,
+                    )
+            z = sb.tile([P, width, PACK], BF16, name=f"z{piece}", align_bytes=64)
+            nc.vector.tensor_tensor(
+                z[:].rearrange("p (c i) t -> p c t i", i=4),
+                larger[:].rearrange("p t (c i) -> p c t i", i=4),
+                gn_sb[:].unsqueeze(1).unsqueeze(3).to_broadcast([P, width // 4, PACK, 4]),
+                ALU.mult,
+            )
+            z_codes = sb.tile([P, width], U32, name=f"z_codes{piece}", align_bytes=64)
+            z_plane = sb.tile([P, width], U8, name=f"z_plane{piece}", align_bytes=64)
+            nc.vector.quantize_mx(out=z_codes[:].bitcast(FP8X4), scales=z_plane[:], in_=z[:].rearrange("p j t -> p (j t)"))
+            for t in range(PACK):
+                rows = slice(P * t, P * (t + 1))
+                nc.tensor.matmul_mx(
+                    out=h2_banks[t][:, cols], lhsT=w1_codes[:, rows].bitcast(FP8X4), lhsT_scale=w_planes[:, rows],
+                    rhs=z_codes[:].bitcast(FP8X4), rhs_scale=z_plane[:], start=False, stop=start + width == S,
+                )
+
+        ea = sb.tile([P, PACK, S], F32, name="ea")
+        top = sb.tile([P, PACK], F32, name="top")
+        ea_bias = sb.tile([P, PACK], F32, name="ea_bias")
+        for t in range(PACK):
+            nc.vector.tensor_scalar(
+                h2_rows[t][:], h2_banks[t][:], 1.0, None, ALU.mult, ALU.max, accum_out=top[:, t : t + 1]
+            )
+            nc.vector.tensor_scalar(ea_bias[:, t : t + 1], top[:, t : t + 1], tau_sb[:, t : t + 1], -1.0, ALU.mult, ALU.mult)
+            for start, width in HALVES:
+                nc.scalar.activation(
+                    ea[:, t, start : start + width], h2_rows[t][:].indirect(entries(n4_sb, start, width)), ACT.Exp,
+                    bias=ea_bias[:, t : t + 1], scale=tau_sb[:, t : t + 1],
+                )
+        h2_n3 = sb.tile([P, PACK, S], F32, name="h2_n3")
+        diff = sb.tile([P, PACK, S], F32, name="diff")
+        for start, width in HALVES:
+            cols = slice(start, start + width)
+            for t in range(PACK):
+                nc.vector.tensor_copy(h2_n3[:, t, cols], h2_rows[t][:].indirect(entries(n3_sb, start, width)))
+            for t in range(PACK):
+                nc.vector.tensor_tensor(diff[:, t, cols], h2_banks[t][:, cols], h2_n3[:, t, cols], ALU.subtract)
+
+        out_rows = out_0.rearrange("(p t) j -> p t j", t=PACK)
+        out_words = words_of(out_1)
+        y_plane = sb.tile([P, S], U8, name="y_plane", align_bytes=64)
+        for piece, (start, width) in enumerate(OUT_PIECES):
+            cols = slice(start, start + width)
+            root = sb.tile([P, PACK, width], F32, name=f"root{piece}")
+            nc.scalar.activation(root[:], ea[:, :, cols], ACT.Abs_reciprocal_sqrt, bias=0.5, scale=2.0)
+            factor = sb.tile([P, PACK, width], F32, name=f"factor{piece}")
+            nc.scalar.activation(factor[:], root[:], ACT.Square)
+            y = sb.tile([P, PACK, width], F32, name=f"y{piece}")
+            nc.vector.tensor_tensor(y[:], diff[:, :, cols], factor[:], ALU.mult)
+            nc.sync.dma_start(out_rows[:, :, cols], y[:])
+            y_bf = sb.tile([P, width, PACK], BF16, name=f"y_bf{piece}", align_bytes=64)
+            nc.vector.tensor_copy(
+                y_bf[:].rearrange("p (c i) t -> p c t i", i=4), y[:].rearrange("p t (c i) -> p c t i", i=4)
+            )
+            y_codes = sb.tile([P, width], U32, name=f"y_codes{piece}", align_bytes=64)
+            nc.vector.quantize_mx(out=y_codes[:].bitcast(FP8X4), scales=y_plane[:, cols], in_=y_bf[:].rearrange("p j t -> p (j t)"))
+            nc.sync.dma_start(out_words[:, cols], y_codes[:].bitcast(I32))
+        for q in range(4):
+            queue = nc.scalar if q % 2 else nc.sync
+            queue.dma_start(out_2[0, 4 * q : 4 * q + 4, :].bitcast(I32), y_plane[32 * q : 32 * q + 4, :].bitcast(I32))

@@ -61,6 +61,11 @@ def tile_picked_pqmixemoera_none_po_kernel(
         dk_plane = sb.tile([P, S], U8, name="dk_plane", align_bytes=64)
         nc.gpsimd.memset(dk_plane[:].bitcast(I32), 0)
 
+        warm_in = sb.tile([P, 1], F32, name="warm_in")
+        nc.vector.memset(warm_in[:], 0.0)
+        warm_sigmoid = sb.tile([P, 1], F32, name="warm_sigmoid")
+        nc.scalar.activation(warm_sigmoid[:], warm_in[:], ACT.Sigmoid)
+
         k1_sb = load_list(k1, "k1_sb")
         d_bytes = sb.tile([P, G], U8, name="d_bytes")
         nc.sync.dma_start(
@@ -174,6 +179,9 @@ def tile_picked_pqmixemoera_none_po_kernel(
                 nc.scalar.activation(h_n2[:, t, :], h_rows[t][:].indirect(entries(n2_sb, start, width)), ACT.Copy)
                 nc.vector.tensor_tensor(gated[:, t, :], h_rows[t][:, cols], sg[:, t, :], ALU.mult)
                 nc.vector.scalar_tensor_tensor(larger[:, t, :], h_n2[:, t, :], 0.75, gated[:, t, :], ALU.mult, ALU.max)
+            if start + width == S:
+                warm_exp = sb.tile([P, 1], F32, name="warm_exp")
+                nc.scalar.activation(warm_exp[:], sg[:, PACK - 1, :1], ACT.Exp)
             if piece == 0:
                 w_planes = sb.tile([P, S], U8, name="w_planes", tag="w_planes", align_bytes=64)
                 deal(nc.vector.tensor_copy, w_planes[:], w_bytes[:])

@@ -19,7 +19,6 @@ FLOPS = 3 * 2 * 512 * 512 * 512
 
 Z_PIECES = ((0, 256), (256, 128), (384, 128))
 HALVES = ((0, 256), (256, 256))
-OUT_PIECES = ((0, 128), (128, 128), (256, 128), (384, 128))
 
 
 def words_of(dram):
@@ -30,10 +29,10 @@ def entries(offsets, start, width):
     return offsets[:, start // 16 : (start + width) // 16]
 
 
-def deal(copy, dst, src):
+def deal(copy, dst, src, run):
     copy(
-        out=dst.rearrange("p (t c i) -> p c t i", t=PACK, i=4),
-        in_=src.rearrange("p (c i t) -> p c t i", t=PACK, i=4),
+        out=dst.rearrange("p (t c i) -> p c t i", t=PACK, i=run),
+        in_=src.rearrange("p (c i t) -> p c t i", t=PACK, i=run),
     )
 
 
@@ -46,6 +45,7 @@ def tile_picked_pqmixemoera_none_po_kernel(
         lists = ctx.enter_context(tc.tile_pool(name="lists", bufs=1))
         sb = ctx.enter_context(tc.tile_pool(name="sb", bufs=1))
         shared = ctx.enter_context(tc.tile_pool(name="shared", bufs=1))
+        tail = ctx.enter_context(tc.tile_pool(name="tail", bufs=1))
         psum = ctx.enter_context(tc.psum_pool(name="psum", bufs=1))
 
         def load_list(dram, name):
@@ -66,6 +66,8 @@ def tile_picked_pqmixemoera_none_po_kernel(
         warm_sigmoid = sb.tile([P, 1], F32, name="warm_sigmoid")
         nc.scalar.activation(warm_sigmoid[:], warm_in[:], ACT.Sigmoid)
 
+        h2_rows = [sb.tile([P, 2 * S], F32, name=f"h2_rows{t}") for t in range(PACK)]
+
         k1_sb = load_list(k1, "k1_sb")
         d_bytes = sb.tile([P, G], U8, name="d_bytes")
         nc.sync.dma_start(
@@ -75,7 +77,7 @@ def tile_picked_pqmixemoera_none_po_kernel(
         offs_sb = load_list(offs, "offs_sb")
         x_bytes = sb.tile([P, T], U8, name="x_bytes")
         for q in range(4):
-            nc.sync.dma_start(
+            nc.scalar.dma_start(
                 x_bytes[32 * q : 32 * q + 32, :].bitcast(I32),
                 x_scales[0, 4 * q : 4 * q + 4, :].bitcast(I32).unsqueeze(0).to_broadcast([8, 4, T // 4]),
             )
@@ -85,10 +87,10 @@ def tile_picked_pqmixemoera_none_po_kernel(
         n2_sb = load_list(n2, "n2_sb")
         two_sb = load_list(two, "two_sb")
         n3_sb = load_list(n3, "n3_sb")
-        x_table = sb.tile([P, T], I32, name="x_table")
-        nc.sync.dma_start(x_table[:], words_of(x_words))
         w2_raw = sb.tile([P, S], I32, name="w2_raw")
         nc.sync.dma_start(w2_raw[:], words_of(w2_words))
+        x_table = sb.tile([P, T], I32, name="x_table")
+        nc.sync.dma_start(x_table[:], words_of(x_words))
         w1_raw = sb.tile([P, S], I32, name="w1_raw")
         nc.sync.dma_start(w1_raw[:], words_of(w1_words))
         n4_sb = load_list(n4, "n4_sb")
@@ -104,7 +106,7 @@ def tile_picked_pqmixemoera_none_po_kernel(
         dk_bytes = sb.tile([P, S], U8, name="dk_bytes", tag="w1_codes", align_bytes=64)
         nc.vector.tensor_copy(dk_bytes[:], d_bytes[:].indirect(k1_sb[:]))
         dk_dealt = sb.tile([P, S], U8, name="dk_dealt", tag="w2_codes", align_bytes=64)
-        deal(nc.vector.tensor_copy, dk_dealt[:], dk_bytes[:])
+        deal(nc.vector.tensor_copy, dk_dealt[:], dk_bytes[:], 16)
         for q in range(4):
             nc.scalar.dma_start(
                 dk_plane[32 * q : 32 * q + 4, :].bitcast(I32),
@@ -125,9 +127,9 @@ def tile_picked_pqmixemoera_none_po_kernel(
             )
 
         w2_codes = sb.tile([P, S], U32, name="w2_codes", tag="w2_codes", align_bytes=64)
-        deal(nc.scalar.copy, w2_codes[:], w2_raw[:].bitcast(U32))
+        deal(nc.scalar.copy, w2_codes[:], w2_raw[:].bitcast(U32), 4)
         w1_codes = sb.tile([P, S], U32, name="w1_codes", tag="w1_codes", align_bytes=64)
-        deal(nc.scalar.copy, w1_codes[:], w1_raw[:].bitcast(U32))
+        deal(nc.scalar.copy, w1_codes[:], w1_raw[:].bitcast(U32), 4)
 
         w_bytes = shared.tile([P, S], U8, name="w_bytes", align_bytes=64, offset=8192)
         nc.gpsimd.memset(w_bytes[:].bitcast(I32), 0)
@@ -141,7 +143,7 @@ def tile_picked_pqmixemoera_none_po_kernel(
         h_rows = [sb.tile([P, S], F32, name=f"h_rows{t}") for t in range(PACK)]
 
         def first_product(t, start, width, bank_name):
-            bank = psum.tile([P, S], F32, name=bank_name)
+            bank = psum.tile([P, S], F32, name=bank_name, bufs=3 if bank_name == "h_bank" else 1)
             rows, cols = slice(P * t, P * (t + 1)), slice(start, start + width)
             nc.tensor.matmul_mx(
                 out=bank[:, :width], lhsT=dk_codes[t][:].bitcast(FP8X4), lhsT_scale=dk_plane[:, rows],
@@ -150,8 +152,8 @@ def tile_picked_pqmixemoera_none_po_kernel(
             return bank[:, :width]
 
         for (start, width), bank_name in zip(HALVES, ("h_first", "h_bank")):
-            nc.vector.tensor_scalar(
-                h_rows[0][:, start : start + width], first_product(0, start, width, bank_name), 0.0625, None, ALU.mult
+            nc.scalar.activation(
+                h_rows[0][:, start : start + width], first_product(0, start, width, bank_name), ACT.Copy, scale=0.0625
             )
         for t in range(1, PACK):
             nc.vector.tensor_copy(dk_codes[t][:], dk_words[:].bitcast(I32)[:, t::PACK])
@@ -162,29 +164,35 @@ def tile_picked_pqmixemoera_none_po_kernel(
         nc.vector.tensor_copy(x2_plane[:], x_bytes[:].indirect(two_sb[:]))
 
         h2_banks = [psum.tile([P, S], F32, name=f"h2_bank{t}") for t in range(PACK)]
-        h2_rows = [sb.tile([P, S], F32, name=f"h2_rows{t}") for t in range(PACK)]
         for piece, (start, width) in enumerate(Z_PIECES):
             cols = slice(start, start + width)
-            sg = sb.tile([P, PACK, width], F32, name=f"sg{piece}")
+            sg = [h2_rows[t][:, S + start : S + start + width] for t in range(PACK)]
             h_n2 = sb.tile([P, PACK, width], F32, name=f"h_n2{piece}")
             gated = sb.tile([P, PACK, width], F32, name=f"gated{piece}")
             larger = sb.tile([P, PACK, width], F32, name=f"larger{piece}")
+            z_rows = sb.tile([P, PACK, width], BF16, name=f"z_rows{piece}")
+            first_open = 0
             for t in range(PACK):
                 if piece == 0 and t > 0:
                     nc.scalar.activation(h_rows[t][:], first_product(t, 0, S, "h_bank"), ACT.Copy, scale=0.0625)
                 nc.scalar.activation(
-                    sg[:, t, :], h_rows[t][:].indirect(entries(n1_sb, start, width)), ACT.Sigmoid,
+                    sg[t], h_rows[t][:].indirect(entries(n1_sb, start, width)), ACT.Sigmoid,
                     bias=sg_bias[:, t : t + 1], scale=sl_sb[:, t : t + 1],
                 )
                 nc.scalar.activation(h_n2[:, t, :], h_rows[t][:].indirect(entries(n2_sb, start, width)), ACT.Copy)
-                nc.vector.tensor_tensor(gated[:, t, :], h_rows[t][:, cols], sg[:, t, :], ALU.mult)
-                nc.vector.scalar_tensor_tensor(larger[:, t, :], h_n2[:, t, :], 0.75, gated[:, t, :], ALU.mult, ALU.max)
+                nc.vector.tensor_tensor(gated[:, t, :], h_rows[t][:, cols], sg[t], ALU.mult)
+                if t == PACK - 1 or (t == PACK - 2 and start + width == S):
+                    done = slice(first_open, t + 1)
+                    nc.vector.scalar_tensor_tensor(larger[:, done, :], h_n2[:, done, :], 0.75, gated[:, done, :], ALU.mult, ALU.max)
+                    for row in range(first_open, t + 1):
+                        nc.vector.tensor_scalar(z_rows[:, row, :], larger[:, row, :], gn_sb[:, row : row + 1], None, ALU.mult)
+                    first_open = t + 1
             if start + width == S:
                 warm_exp = sb.tile([P, 1], F32, name="warm_exp")
-                nc.scalar.activation(warm_exp[:], sg[:, PACK - 1, :1], ACT.Exp)
+                nc.scalar.activation(warm_exp[:], sg[PACK - 1][:, :1], ACT.Exp)
             if piece == 0:
                 w_planes = sb.tile([P, S], U8, name="w_planes", tag="w_planes", align_bytes=64)
-                deal(nc.vector.tensor_copy, w_planes[:], w_bytes[:])
+                deal(nc.vector.tensor_copy, w_planes[:], w_bytes[:], 16)
                 for t in range(PACK):
                     rows = slice(P * t, P * (t + 1))
                     nc.tensor.matmul_mx(
@@ -192,12 +200,7 @@ def tile_picked_pqmixemoera_none_po_kernel(
                         rhs=x2_codes[:].bitcast(FP8X4), rhs_scale=x2_plane[:], start=True, stop=False,
                     )
             z = sb.tile([P, width, PACK], BF16, name=f"z{piece}", align_bytes=64)
-            nc.vector.tensor_tensor(
-                z[:].rearrange("p (c i) t -> p c t i", i=4),
-                larger[:].rearrange("p t (c i) -> p c t i", i=4),
-                gn_sb[:].unsqueeze(1).unsqueeze(3).to_broadcast([P, width // 4, PACK, 4]),
-                ALU.mult,
-            )
+            nc.vector.tensor_copy(z[:], z_rows[:].rearrange("p t j -> p j t"))
             z_codes = sb.tile([P, width], U32, name=f"z_codes{piece}", align_bytes=64)
             z_plane = sb.tile([P, width], U8, name=f"z_plane{piece}", align_bytes=64)
             nc.vector.quantize_mx(out=z_codes[:].bitcast(FP8X4), scales=z_plane[:], in_=z[:].rearrange("p j t -> p (j t)"))
@@ -211,44 +214,62 @@ def tile_picked_pqmixemoera_none_po_kernel(
         ea = sb.tile([P, PACK, S], F32, name="ea")
         top = sb.tile([P, PACK], F32, name="top")
         ea_bias = sb.tile([P, PACK], F32, name="ea_bias")
-        for t in range(PACK):
-            nc.vector.tensor_scalar(
-                h2_rows[t][:], h2_banks[t][:], 1.0, None, ALU.mult, ALU.max, accum_out=top[:, t : t + 1]
-            )
-            nc.vector.tensor_scalar(ea_bias[:, t : t + 1], top[:, t : t + 1], tau_sb[:, t : t + 1], -1.0, ALU.mult, ALU.mult)
-            for start, width in HALVES:
-                nc.scalar.activation(
-                    ea[:, t, start : start + width], h2_rows[t][:].indirect(entries(n4_sb, start, width)), ACT.Exp,
-                    bias=ea_bias[:, t : t + 1], scale=tau_sb[:, t : t + 1],
-                )
         h2_n3 = sb.tile([P, PACK, S], F32, name="h2_n3")
         diff = sb.tile([P, PACK, S], F32, name="diff")
-        for start, width in HALVES:
-            cols = slice(start, start + width)
-            for t in range(PACK):
-                nc.vector.tensor_copy(h2_n3[:, t, cols], h2_rows[t][:].indirect(entries(n3_sb, start, width)))
-            for t in range(PACK):
-                nc.vector.tensor_tensor(diff[:, t, cols], h2_banks[t][:, cols], h2_n3[:, t, cols], ALU.subtract)
+
+        def leave_bank(t):
+            nc.vector.tensor_scalar(
+                h2_rows[t][:, :S], h2_banks[t][:], 1.0, None, ALU.mult, ALU.max, accum_out=top[:, t : t + 1]
+            )
+
+        def exponential(t):
+            nc.vector.tensor_scalar(ea_bias[:, t : t + 1], top[:, t : t + 1], tau_sb[:, t : t + 1], -1.0, ALU.mult, ALU.mult)
+            nc.scalar.activation(
+                ea[:, t, :], h2_rows[t][:].indirect(n4_sb[:]), ACT.Exp, bias=ea_bias[:, t : t + 1], scale=tau_sb[:, t : t + 1]
+            )
+
+        leave_bank(0)
+        exponential(0)
+        leave_bank(1)
+        for t in range(1, PACK):
+            if t + 1 < PACK:
+                leave_bank(t + 1)
+            exponential(t)
+        for t in range(PACK + 1):
+            if t < PACK:
+                nc.vector.tensor_copy(h2_n3[:, t, :], h2_rows[t][:].indirect(n3_sb[:]))
+            if t > 0:
+                nc.vector.tensor_tensor(diff[:, t - 1, :], h2_banks[t - 1][:], h2_n3[:, t - 1, :], ALU.subtract)
 
         out_rows = out_0.rearrange("(p t) j -> p t j", t=PACK)
         out_words = words_of(out_1)
         y_plane = sb.tile([P, S], U8, name="y_plane", align_bytes=64)
-        for piece, (start, width) in enumerate(OUT_PIECES):
-            cols = slice(start, start + width)
-            root = sb.tile([P, PACK, width], F32, name=f"root{piece}")
-            nc.scalar.activation(root[:], ea[:, :, cols], ACT.Abs_reciprocal_sqrt, bias=0.5, scale=2.0)
-            factor = sb.tile([P, PACK, width], F32, name=f"factor{piece}")
-            nc.scalar.activation(factor[:], root[:], ACT.Square)
-            y = sb.tile([P, PACK, width], F32, name=f"y{piece}")
-            nc.vector.tensor_tensor(y[:], diff[:, :, cols], factor[:], ALU.mult)
-            nc.sync.dma_start(out_rows[:, :, cols], y[:])
-            y_bf = sb.tile([P, width, PACK], BF16, name=f"y_bf{piece}", align_bytes=64)
-            nc.vector.tensor_copy(
-                y_bf[:].rearrange("p (c i) t -> p c t i", i=4), y[:].rearrange("p t (c i) -> p c t i", i=4)
-            )
-            y_codes = sb.tile([P, width], U32, name=f"y_codes{piece}", align_bytes=64)
-            nc.vector.quantize_mx(out=y_codes[:].bitcast(FP8X4), scales=y_plane[:, cols], in_=y_bf[:].rearrange("p j t -> p (j t)"))
-            nc.sync.dma_start(out_words[:, cols], y_codes[:].bitcast(I32))
+        width = 128
+        count = S // width
+        cols = [slice(c * width, (c + 1) * width) for c in range(count)]
+        slot = PACK * width * 4
+        roots, factors, ys, y_bfs = [], [], [], []
+        for c in range(count + 1):
+            if c < count:
+                roots.append(tail.tile([P, PACK, width], F32, name=f"root{c}", align_bytes=64, offset=c * slot))
+                nc.scalar.activation(roots[c][:], ea[:, :, cols[c]], ACT.Abs_reciprocal_sqrt, bias=0.5, scale=2.0)
+            if c > 0:
+                factors.append(sb.tile([P, PACK, width], F32, name=f"factor{c - 1}"))
+                nc.scalar.activation(factors[c - 1][:], roots[c - 1][:], ACT.Square)
+        for c in range(count + 2):
+            if c < count:
+                ys.append(sb.tile([P, PACK, width], F32, name=f"y{c}"))
+                nc.vector.tensor_tensor(ys[c][:], diff[:, :, cols[c]], factors[c][:], ALU.mult)
+                nc.sync.dma_start(out_rows[:, :, cols[c]], ys[c][:])
+            if 1 <= c <= count:
+                y_bfs.append(tail.tile([P, width, PACK], BF16, name=f"y_bf{c - 1}", align_bytes=64, offset=c * slot))
+                nc.vector.tensor_copy(y_bfs[c - 1][:], ys[c - 1][:].rearrange("p t j -> p j t"))
+            if c >= 2:
+                y_codes = tail.tile([P, width], U32, name=f"y_codes{c - 2}", align_bytes=64, offset=c * slot + slot // 2)
+                nc.vector.quantize_mx(
+                    out=y_codes[:].bitcast(FP8X4), scales=y_plane[:, cols[c - 2]], in_=y_bfs[c - 2][:].rearrange("p j t -> p (j t)")
+                )
+                nc.sync.dma_start(out_words[:, cols[c - 2]], y_codes[:].bitcast(I32))
         for q in range(4):
             queue = nc.scalar if q % 2 else nc.sync
             queue.dma_start(out_2[0, 4 * q : 4 * q + 4, :].bitcast(I32), y_plane[32 * q : 32 * q + 4, :].bitcast(I32))

@@ -58,9 +58,6 @@ def tile_picked_pqmixemoera_none_po_kernel(
             nc.gpsimd.dma_start(column[:], dram.rearrange("(p t) o -> p (t o)", t=PACK))
             return column
 
-        dk_plane = sb.tile([P, S], U8, name="dk_plane", align_bytes=64)
-        nc.gpsimd.memset(dk_plane[:].bitcast(I32), 0)
-
         warm_in = sb.tile([P, 1], F32, name="warm_in")
         nc.vector.memset(warm_in[:], 0.0)
         warm_sigmoid = sb.tile([P, 1], F32, name="warm_sigmoid")
@@ -77,23 +74,21 @@ def tile_picked_pqmixemoera_none_po_kernel(
         offs_sb = load_list(offs, "offs_sb")
         x_bytes = sb.tile([P, T], U8, name="x_bytes")
         for q in range(4):
-            nc.scalar.dma_start(
+            (nc.scalar if q < 3 else nc.sync).dma_start(
                 x_bytes[32 * q : 32 * q + 32, :].bitcast(I32),
                 x_scales[0, 4 * q : 4 * q + 4, :].bitcast(I32).unsqueeze(0).to_broadcast([8, 4, T // 4]),
             )
-        d_table = shared.tile([P, G], I32, name="d_table", align_bytes=64, offset=4096)
+        d_table = shared.tile([P, G], I32, name="d_table", align_bytes=64, offset=8192)
         nc.sync.dma_start(d_table[:], words_of(d_words))
-        n1_sb = load_list(n1, "n1_sb")
-        n2_sb = load_list(n2, "n2_sb")
-        two_sb = load_list(two, "two_sb")
-        n3_sb = load_list(n3, "n3_sb")
         w2_raw = sb.tile([P, S], I32, name="w2_raw")
         nc.sync.dma_start(w2_raw[:], words_of(w2_words))
         x_table = sb.tile([P, T], I32, name="x_table")
         nc.sync.dma_start(x_table[:], words_of(x_words))
         w1_raw = sb.tile([P, S], I32, name="w1_raw")
         nc.sync.dma_start(w1_raw[:], words_of(w1_words))
-        n4_sb = load_list(n4, "n4_sb")
+        n1_sb = load_list(n1, "n1_sb")
+        n2_sb = load_list(n2, "n2_sb")
+        two_sb = load_list(two, "two_sb")
         sl_sb = load_rows(sl, "sl_sb")
         th_sb = load_rows(th, "th_sb")
         sl_th = sb.tile([P, PACK], F32, name="sl_th")
@@ -103,42 +98,40 @@ def tile_picked_pqmixemoera_none_po_kernel(
         gn_sb = load_rows(gn, "gn_sb")
         tau_sb = load_rows(tau, "tau_sb")
 
-        dk_bytes = sb.tile([P, S], U8, name="dk_bytes", tag="w1_codes", align_bytes=64)
+        dk_bytes = sb.tile([P, S], U8, name="dk_bytes", tag="w_bytes")
         nc.vector.tensor_copy(dk_bytes[:], d_bytes[:].indirect(k1_sb[:]))
-        dk_dealt = sb.tile([P, S], U8, name="dk_dealt", tag="w2_codes", align_bytes=64)
-        deal(nc.vector.tensor_copy, dk_dealt[:], dk_bytes[:], 16)
-        for q in range(4):
-            nc.scalar.dma_start(
-                dk_plane[32 * q : 32 * q + 4, :].bitcast(I32),
-                dk_dealt[32 * q : 32 * q + 32 : 8, :].bitcast(I32),
-            )
+        dk_plane = sb.tile([P, S], U8, name="dk_plane", align_bytes=64)
+        deal(nc.vector.tensor_copy, dk_plane[:], dk_bytes[:], 16)
+        for a in range(1, 4):
+            nc.scalar.dma_start(dk_plane[a:P:32, :].bitcast(I32), dk_plane[8 * a : P : 32, :].bitcast(I32))
+        w_bytes = sb.tile([P, S], U8, name="w_bytes", tag="w_bytes")
+        nc.gpsimd.memset(w_bytes[:].bitcast(I32), 0)
+        for place, scales, queue in ((4, w2_scales, nc.sync), (0, w1_scales, nc.gpsimd)):
+            for q in range(4):
+                queue.dma_start(
+                    w_bytes[32 * q + place : 32 * q + place + 4, :].bitcast(I32),
+                    scales[0, 4 * q : 4 * q + 4, :].bitcast(I32),
+                )
+        n4_sb = load_list(n4, "n4_sb")
+        n3_sb = load_list(n3, "n3_sb")
         xq_plane = sb.tile([P, S], U8, name="xq_plane", align_bytes=64)
         nc.vector.tensor_copy(xq_plane[:], x_bytes[:].indirect(offs_sb[:]))
         dk_words = sb.tile([P, S], U32, name="dk_words")
         nc.vector.tensor_copy(dk_words[:], d_table[:].bitcast(U32).indirect(k1_sb[:]))
         dk_codes = [shared.tile([P, P], I32, name="dk_codes0", align_bytes=64, offset=1792)]
-        dk_codes.extend(sb.tile([P, P], I32, name=f"dk_codes{t}", align_bytes=64) for t in range(1, PACK - 1))
-        dk_codes.append(sb.tile([P, P], I32, name="dk_codes3", tag="w_planes", align_bytes=64))
+        for t, heir in ((1, "dk_codes1"), (2, "dk_codes2"), (3, "w_planes")):
+            dk_codes.append(sb.tile([P, P], I32, name=f"dk_codes{t}", tag=heir, align_bytes=64))
         nc.vector.tensor_copy(dk_codes[0][:], dk_words[:].bitcast(I32)[:, 0::PACK])
-        xq_codes = shared.tile([P, S], U32, name="xq_codes", align_bytes=64, offset=4096)
+        xq_codes = shared.tile([P, S], U32, name="xq_codes", align_bytes=64, offset=8192)
         for start, width in HALVES:
             nc.vector.tensor_copy(
                 xq_codes[:, start : start + width], x_table[:].bitcast(U32).indirect(entries(offs_sb, start, width))
             )
 
-        w2_codes = sb.tile([P, S], U32, name="w2_codes", tag="w2_codes", align_bytes=64)
+        w2_codes = sb.tile([P, S], U32, name="w2_codes", align_bytes=64)
         deal(nc.scalar.copy, w2_codes[:], w2_raw[:].bitcast(U32), 4)
-        w1_codes = sb.tile([P, S], U32, name="w1_codes", tag="w1_codes", align_bytes=64)
+        w1_codes = sb.tile([P, S], U32, name="w1_codes", align_bytes=64)
         deal(nc.scalar.copy, w1_codes[:], w1_raw[:].bitcast(U32), 4)
-
-        w_bytes = shared.tile([P, S], U8, name="w_bytes", align_bytes=64, offset=8192)
-        nc.gpsimd.memset(w_bytes[:].bitcast(I32), 0)
-        for place, scales in ((4, w2_scales), (0, w1_scales)):
-            for q in range(4):
-                nc.sync.dma_start(
-                    w_bytes[32 * q + place : 32 * q + place + 4, :].bitcast(I32),
-                    scales[0, 4 * q : 4 * q + 4, :].bitcast(I32),
-                )
 
         h_rows = [sb.tile([P, S], F32, name=f"h_rows{t}") for t in range(PACK)]
 
@@ -158,49 +151,52 @@ def tile_picked_pqmixemoera_none_po_kernel(
         for t in range(1, PACK):
             nc.vector.tensor_copy(dk_codes[t][:], dk_words[:].bitcast(I32)[:, t::PACK])
 
+        nc.scalar.activation(h_rows[1][:], first_product(1, 0, S, "h_bank"), ACT.Copy, scale=0.0625)
+        for t in range(2, PACK):
+            nc.vector.tensor_scalar(h_rows[t][:], first_product(t, 0, S, "h_bank"), 0.0625, None, ALU.mult)
+
         x2_codes = shared.tile([P, S], U32, name="x2_codes", align_bytes=64, offset=0)
         nc.vector.tensor_copy(x2_codes[:], x_table[:].bitcast(U32).indirect(two_sb[:]))
         x2_plane = shared.tile([P, S], U8, name="x2_plane", align_bytes=64, offset=2048)
         nc.vector.tensor_copy(x2_plane[:], x_bytes[:].indirect(two_sb[:]))
 
         h2_banks = [psum.tile([P, S], F32, name=f"h2_bank{t}") for t in range(PACK)]
+        w_planes = sb.tile([P, S], U8, name="w_planes", tag="w_planes", align_bytes=64)
+        deal(nc.vector.tensor_copy, w_planes[:], w_bytes[:], 16)
+        for t in range(PACK):
+            rows = slice(P * t, P * (t + 1))
+            nc.tensor.matmul_mx(
+                out=h2_banks[t][:], lhsT=w2_codes[:, rows].bitcast(FP8X4), lhsT_scale=w_planes[4:P, rows],
+                rhs=x2_codes[:].bitcast(FP8X4), rhs_scale=x2_plane[:], start=True, stop=False,
+            )
         for piece, (start, width) in enumerate(Z_PIECES):
             cols = slice(start, start + width)
             sg = [h2_rows[t][:, S + start : S + start + width] for t in range(PACK)]
             h_n2 = sb.tile([P, PACK, width], F32, name=f"h_n2{piece}")
             gated = sb.tile([P, PACK, width], F32, name=f"gated{piece}")
             larger = sb.tile([P, PACK, width], F32, name=f"larger{piece}")
-            z_rows = sb.tile([P, PACK, width], BF16, name=f"z_rows{piece}")
             first_open = 0
             for t in range(PACK):
-                if piece == 0 and t > 0:
-                    nc.scalar.activation(h_rows[t][:], first_product(t, 0, S, "h_bank"), ACT.Copy, scale=0.0625)
                 nc.scalar.activation(
                     sg[t], h_rows[t][:].indirect(entries(n1_sb, start, width)), ACT.Sigmoid,
                     bias=sg_bias[:, t : t + 1], scale=sl_sb[:, t : t + 1],
                 )
                 nc.scalar.activation(h_n2[:, t, :], h_rows[t][:].indirect(entries(n2_sb, start, width)), ACT.Copy)
                 nc.vector.tensor_tensor(gated[:, t, :], h_rows[t][:, cols], sg[t], ALU.mult)
-                if t == PACK - 1 or (t == PACK - 2 and start + width == S):
+                if piece == 0 or t == PACK - 1 or (t == PACK - 2 and start + width == S):
                     done = slice(first_open, t + 1)
                     nc.vector.scalar_tensor_tensor(larger[:, done, :], h_n2[:, done, :], 0.75, gated[:, done, :], ALU.mult, ALU.max)
-                    for row in range(first_open, t + 1):
-                        nc.vector.tensor_scalar(z_rows[:, row, :], larger[:, row, :], gn_sb[:, row : row + 1], None, ALU.mult)
                     first_open = t + 1
             if start + width == S:
                 warm_exp = sb.tile([P, 1], F32, name="warm_exp")
                 nc.scalar.activation(warm_exp[:], sg[PACK - 1][:, :1], ACT.Exp)
-            if piece == 0:
-                w_planes = sb.tile([P, S], U8, name="w_planes", tag="w_planes", align_bytes=64)
-                deal(nc.vector.tensor_copy, w_planes[:], w_bytes[:], 16)
-                for t in range(PACK):
-                    rows = slice(P * t, P * (t + 1))
-                    nc.tensor.matmul_mx(
-                        out=h2_banks[t][:], lhsT=w2_codes[:, rows].bitcast(FP8X4), lhsT_scale=w_planes[4:P, rows],
-                        rhs=x2_codes[:].bitcast(FP8X4), rhs_scale=x2_plane[:], start=True, stop=False,
-                    )
             z = sb.tile([P, width, PACK], BF16, name=f"z{piece}", align_bytes=64)
-            nc.vector.tensor_copy(z[:], z_rows[:].rearrange("p t j -> p j t"))
+            nc.vector.tensor_tensor(
+                z[:].rearrange("p (c i) t -> p c t i", i=4),
+                larger[:].rearrange("p t (c i) -> p c t i", i=4),
+                gn_sb[:].unsqueeze(1).unsqueeze(3).to_broadcast([P, width // 4, PACK, 4]),
+                ALU.mult,
+            )
             z_codes = sb.tile([P, width], U32, name=f"z_codes{piece}", align_bytes=64)
             z_plane = sb.tile([P, width], U8, name=f"z_plane{piece}", align_bytes=64)
             nc.vector.quantize_mx(out=z_codes[:].bitcast(FP8X4), scales=z_plane[:], in_=z[:].rearrange("p j t -> p (j t)"))
@@ -223,7 +219,7 @@ def tile_picked_pqmixemoera_none_po_kernel(
             )
 
         def exponential(t):
-            nc.vector.tensor_scalar(ea_bias[:, t : t + 1], top[:, t : t + 1], tau_sb[:, t : t + 1], -1.0, ALU.mult, ALU.mult)
+            nc.gpsimd.tensor_scalar(ea_bias[:, t : t + 1], top[:, t : t + 1], tau_sb[:, t : t + 1], -1.0, ALU.mult, ALU.mult)
             nc.scalar.activation(
                 ea[:, t, :], h2_rows[t][:].indirect(n4_sb[:]), ACT.Exp, bias=ea_bias[:, t : t + 1], scale=tau_sb[:, t : t + 1]
             )

@@ -14,11 +14,23 @@ ACT = mybir.ActivationFunctionType
 
 P = 128
 PACK = 4
-T, S, G = 1024, 512, 2048
+QUADRANTS = 4
+T, G = 1024, 2048
+S = 512
+N = 512
 FLOPS = 3 * 2 * 512 * 512 * 512
 
-Z_PIECES = ((0, 256), (256, 128), (384, 128))
+WORD_RUN, BYTE_RUN = 4, 16
+W2_PLANE = 4
+
 HALVES = ((0, 256), (256, 256))
+Z_PIECES = ((0, 256), (256, 128), (384, 128))
+MAX_RUNS = (((0, 1), (1, 2), (2, 3), (3, 4)), ((0, 4),), ((0, 3), (3, 4)))
+OUT_WIDTH = 128
+
+X2_CODES_AT, X2_PLANE_AT = 0, 2048
+DK_FIRST_AT = X2_PLANE_AT - 256
+D_TABLE_AT = 8192
 
 
 def words_of(dram):
@@ -45,7 +57,6 @@ def tile_picked_pqmixemoera_none_po_kernel(
         lists = ctx.enter_context(tc.tile_pool(name="lists", bufs=1))
         sb = ctx.enter_context(tc.tile_pool(name="sb", bufs=1))
         shared = ctx.enter_context(tc.tile_pool(name="shared", bufs=1))
-        tail = ctx.enter_context(tc.tile_pool(name="tail", bufs=1))
         psum = ctx.enter_context(tc.psum_pool(name="psum", bufs=1))
 
         def load_list(dram, name):
@@ -54,9 +65,9 @@ def tile_picked_pqmixemoera_none_po_kernel(
             return offsets
 
         def load_rows(dram, name):
-            column = sb.tile([P, PACK], F32, name=name)
-            nc.gpsimd.dma_start(column[:], dram.rearrange("(p t) o -> p (t o)", t=PACK))
-            return column
+            values = sb.tile([P, PACK], F32, name=name)
+            nc.gpsimd.dma_start(values[:], dram.rearrange("(p t) o -> p (t o)", t=PACK))
+            return values
 
         warm_in = sb.tile([P, 1], F32, name="warm_in")
         nc.vector.memset(warm_in[:], 0.0)
@@ -73,18 +84,18 @@ def tile_picked_pqmixemoera_none_po_kernel(
         )
         offs_sb = load_list(offs, "offs_sb")
         x_bytes = sb.tile([P, T], U8, name="x_bytes")
-        for q in range(4):
-            (nc.scalar if q < 3 else nc.sync).dma_start(
+        for q in range(QUADRANTS):
+            (nc.scalar if q < QUADRANTS - 1 else nc.sync).dma_start(
                 x_bytes[32 * q : 32 * q + 32, :].bitcast(I32),
                 x_scales[0, 4 * q : 4 * q + 4, :].bitcast(I32).unsqueeze(0).to_broadcast([8, 4, T // 4]),
             )
-        d_table = shared.tile([P, G], I32, name="d_table", align_bytes=64, offset=8192)
+        d_table = shared.tile([P, G], I32, name="d_table", align_bytes=64, offset=D_TABLE_AT)
         nc.sync.dma_start(d_table[:], words_of(d_words))
-        w2_raw = sb.tile([P, S], I32, name="w2_raw")
-        nc.sync.dma_start(w2_raw[:], words_of(w2_words))
         x_table = sb.tile([P, T], I32, name="x_table")
         nc.sync.dma_start(x_table[:], words_of(x_words))
-        w1_raw = sb.tile([P, S], I32, name="w1_raw")
+        w2_raw = sb.tile([P, N], I32, name="w2_raw")
+        nc.sync.dma_start(w2_raw[:], words_of(w2_words))
+        w1_raw = sb.tile([P, N], I32, name="w1_raw")
         nc.sync.dma_start(w1_raw[:], words_of(w1_words))
         n1_sb = load_list(n1, "n1_sb")
         n2_sb = load_list(n2, "n2_sb")
@@ -101,13 +112,13 @@ def tile_picked_pqmixemoera_none_po_kernel(
         dk_bytes = sb.tile([P, S], U8, name="dk_bytes", tag="w_bytes")
         nc.vector.tensor_copy(dk_bytes[:], d_bytes[:].indirect(k1_sb[:]))
         dk_plane = sb.tile([P, S], U8, name="dk_plane", align_bytes=64)
-        deal(nc.vector.tensor_copy, dk_plane[:], dk_bytes[:], 16)
+        deal(nc.vector.tensor_copy, dk_plane[:], dk_bytes[:], BYTE_RUN)
         for a in range(1, 4):
             nc.scalar.dma_start(dk_plane[a:P:32, :].bitcast(I32), dk_plane[8 * a : P : 32, :].bitcast(I32))
-        w_bytes = sb.tile([P, S], U8, name="w_bytes", tag="w_bytes")
+        w_bytes = sb.tile([P, N], U8, name="w_bytes", tag="w_bytes")
         nc.gpsimd.memset(w_bytes[:].bitcast(I32), 0)
-        for place, scales, queue in ((4, w2_scales, nc.sync), (0, w1_scales, nc.gpsimd)):
-            for q in range(4):
+        for place, scales, queue in ((W2_PLANE, w2_scales, nc.sync), (0, w1_scales, nc.gpsimd)):
+            for q in range(QUADRANTS):
                 queue.dma_start(
                     w_bytes[32 * q + place : 32 * q + place + 4, :].bitcast(I32),
                     scales[0, 4 * q : 4 * q + 4, :].bitcast(I32),
@@ -118,20 +129,20 @@ def tile_picked_pqmixemoera_none_po_kernel(
         nc.vector.tensor_copy(xq_plane[:], x_bytes[:].indirect(offs_sb[:]))
         dk_words = sb.tile([P, S], U32, name="dk_words")
         nc.vector.tensor_copy(dk_words[:], d_table[:].bitcast(U32).indirect(k1_sb[:]))
-        dk_codes = [shared.tile([P, P], I32, name="dk_codes0", align_bytes=64, offset=1792)]
-        for t, heir in ((1, "dk_codes1"), (2, "dk_codes2"), (3, "w_planes")):
-            dk_codes.append(sb.tile([P, P], I32, name=f"dk_codes{t}", tag=heir, align_bytes=64))
-        nc.vector.tensor_copy(dk_codes[0][:], dk_words[:].bitcast(I32)[:, 0::PACK])
-        xq_codes = shared.tile([P, S], U32, name="xq_codes", align_bytes=64, offset=8192)
+        dk_first = shared.tile([P, P], I32, name="dk_first", align_bytes=64, offset=DK_FIRST_AT)
+        dk_rest = sb.tile([P, PACK - 1, P], I32, name="dk_rest", tag="w_planes", align_bytes=64)
+        dk_codes = [dk_first[:]] + [dk_rest[:, t, :] for t in range(PACK - 1)]
+        nc.vector.tensor_copy(dk_first[:], dk_words[:].bitcast(I32)[:, 0::PACK])
+        xq_codes = shared.tile([P, S], U32, name="xq_codes", align_bytes=64, offset=D_TABLE_AT)
         for start, width in HALVES:
             nc.vector.tensor_copy(
                 xq_codes[:, start : start + width], x_table[:].bitcast(U32).indirect(entries(offs_sb, start, width))
             )
 
-        w2_codes = sb.tile([P, S], U32, name="w2_codes", align_bytes=64)
-        deal(nc.scalar.copy, w2_codes[:], w2_raw[:].bitcast(U32), 4)
-        w1_codes = sb.tile([P, S], U32, name="w1_codes", align_bytes=64)
-        deal(nc.scalar.copy, w1_codes[:], w1_raw[:].bitcast(U32), 4)
+        w2_codes = sb.tile([P, N], U32, name="w2_codes", align_bytes=64)
+        deal(nc.scalar.copy, w2_codes[:], w2_raw[:].bitcast(U32), WORD_RUN)
+        w1_codes = sb.tile([P, N], U32, name="w1_codes", align_bytes=64)
+        deal(nc.scalar.copy, w1_codes[:], w1_raw[:].bitcast(U32), WORD_RUN)
 
         h_rows = [sb.tile([P, S], F32, name=f"h_rows{t}") for t in range(PACK)]
 
@@ -139,7 +150,7 @@ def tile_picked_pqmixemoera_none_po_kernel(
             bank = psum.tile([P, S], F32, name=bank_name, bufs=3 if bank_name == "h_bank" else 1)
             rows, cols = slice(P * t, P * (t + 1)), slice(start, start + width)
             nc.tensor.matmul_mx(
-                out=bank[:, :width], lhsT=dk_codes[t][:].bitcast(FP8X4), lhsT_scale=dk_plane[:, rows],
+                out=bank[:, :width], lhsT=dk_codes[t].bitcast(FP8X4), lhsT_scale=dk_plane[:, rows],
                 rhs=xq_codes[:, cols].bitcast(FP8X4), rhs_scale=xq_plane[:, cols], start=True, stop=True,
             )
             return bank[:, :width]
@@ -148,53 +159,56 @@ def tile_picked_pqmixemoera_none_po_kernel(
             nc.scalar.activation(
                 h_rows[0][:, start : start + width], first_product(0, start, width, bank_name), ACT.Copy, scale=0.0625
             )
-        for t in range(1, PACK):
-            nc.vector.tensor_copy(dk_codes[t][:], dk_words[:].bitcast(I32)[:, t::PACK])
+        nc.vector.tensor_copy(
+            dk_rest[:].rearrange("p t (c i) -> p c t i", i=WORD_RUN),
+            dk_words[:].bitcast(I32).rearrange("p (c i t) -> p c t i", t=PACK, i=WORD_RUN)[:, :, 1:, :],
+        )
 
         nc.scalar.activation(h_rows[1][:], first_product(1, 0, S, "h_bank"), ACT.Copy, scale=0.0625)
         for t in range(2, PACK):
             nc.vector.tensor_scalar(h_rows[t][:], first_product(t, 0, S, "h_bank"), 0.0625, None, ALU.mult)
 
-        x2_codes = shared.tile([P, S], U32, name="x2_codes", align_bytes=64, offset=0)
+        x2_codes = shared.tile([P, S], U32, name="x2_codes", align_bytes=64, offset=X2_CODES_AT)
         nc.vector.tensor_copy(x2_codes[:], x_table[:].bitcast(U32).indirect(two_sb[:]))
-        x2_plane = shared.tile([P, S], U8, name="x2_plane", align_bytes=64, offset=2048)
+        x2_plane = shared.tile([P, S], U8, name="x2_plane", align_bytes=64, offset=X2_PLANE_AT)
         nc.vector.tensor_copy(x2_plane[:], x_bytes[:].indirect(two_sb[:]))
 
         h2_banks = [psum.tile([P, S], F32, name=f"h2_bank{t}") for t in range(PACK)]
-        w_planes = sb.tile([P, S], U8, name="w_planes", tag="w_planes", align_bytes=64)
-        deal(nc.vector.tensor_copy, w_planes[:], w_bytes[:], 16)
+        w_planes = sb.tile([P, N], U8, name="w_planes", tag="w_planes", align_bytes=64)
+        deal(nc.vector.tensor_copy, w_planes[:], w_bytes[:], BYTE_RUN)
         for t in range(PACK):
             rows = slice(P * t, P * (t + 1))
             nc.tensor.matmul_mx(
-                out=h2_banks[t][:], lhsT=w2_codes[:, rows].bitcast(FP8X4), lhsT_scale=w_planes[4:P, rows],
+                out=h2_banks[t][:], lhsT=w2_codes[:, rows].bitcast(FP8X4), lhsT_scale=w_planes[W2_PLANE:P, rows],
                 rhs=x2_codes[:].bitcast(FP8X4), rhs_scale=x2_plane[:], start=True, stop=False,
             )
+
         for piece, (start, width) in enumerate(Z_PIECES):
             cols = slice(start, start + width)
+            last_piece = start + width == S
             sg = [h2_rows[t][:, S + start : S + start + width] for t in range(PACK)]
             h_n2 = sb.tile([P, PACK, width], F32, name=f"h_n2{piece}")
             gated = sb.tile([P, PACK, width], F32, name=f"gated{piece}")
             larger = sb.tile([P, PACK, width], F32, name=f"larger{piece}")
-            first_open = 0
-            for t in range(PACK):
-                nc.scalar.activation(
-                    sg[t], h_rows[t][:].indirect(entries(n1_sb, start, width)), ACT.Sigmoid,
-                    bias=sg_bias[:, t : t + 1], scale=sl_sb[:, t : t + 1],
+            for first, end in MAX_RUNS[piece]:
+                for t in range(first, end):
+                    nc.scalar.activation(
+                        sg[t], h_rows[t][:].indirect(entries(n1_sb, start, width)), ACT.Sigmoid,
+                        bias=sg_bias[:, t : t + 1], scale=sl_sb[:, t : t + 1],
+                    )
+                    nc.scalar.activation(h_n2[:, t, :], h_rows[t][:].indirect(entries(n2_sb, start, width)), ACT.Copy)
+                    nc.vector.tensor_tensor(gated[:, t, :], h_rows[t][:, cols], sg[t], ALU.mult)
+                nc.vector.scalar_tensor_tensor(
+                    larger[:, first:end, :], h_n2[:, first:end, :], 0.75, gated[:, first:end, :], ALU.mult, ALU.max
                 )
-                nc.scalar.activation(h_n2[:, t, :], h_rows[t][:].indirect(entries(n2_sb, start, width)), ACT.Copy)
-                nc.vector.tensor_tensor(gated[:, t, :], h_rows[t][:, cols], sg[t], ALU.mult)
-                if piece == 0 or t == PACK - 1 or (t == PACK - 2 and start + width == S):
-                    done = slice(first_open, t + 1)
-                    nc.vector.scalar_tensor_tensor(larger[:, done, :], h_n2[:, done, :], 0.75, gated[:, done, :], ALU.mult, ALU.max)
-                    first_open = t + 1
-            if start + width == S:
+            if last_piece:
                 warm_exp = sb.tile([P, 1], F32, name="warm_exp")
                 nc.scalar.activation(warm_exp[:], sg[PACK - 1][:, :1], ACT.Exp)
             z = sb.tile([P, width, PACK], BF16, name=f"z{piece}", align_bytes=64)
             nc.vector.tensor_tensor(
-                z[:].rearrange("p (c i) t -> p c t i", i=4),
-                larger[:].rearrange("p t (c i) -> p c t i", i=4),
-                gn_sb[:].unsqueeze(1).unsqueeze(3).to_broadcast([P, width // 4, PACK, 4]),
+                z[:].rearrange("p (c i) t -> p c t i", i=WORD_RUN),
+                larger[:].rearrange("p t (c i) -> p c t i", i=WORD_RUN),
+                gn_sb[:].unsqueeze(1).unsqueeze(3).to_broadcast([P, width // WORD_RUN, PACK, WORD_RUN]),
                 ALU.mult,
             )
             z_codes = sb.tile([P, width], U32, name=f"z_codes{piece}", align_bytes=64)
@@ -204,7 +218,7 @@ def tile_picked_pqmixemoera_none_po_kernel(
                 rows = slice(P * t, P * (t + 1))
                 nc.tensor.matmul_mx(
                     out=h2_banks[t][:, cols], lhsT=w1_codes[:, rows].bitcast(FP8X4), lhsT_scale=w_planes[:, rows],
-                    rhs=z_codes[:].bitcast(FP8X4), rhs_scale=z_plane[:], start=False, stop=start + width == S,
+                    rhs=z_codes[:].bitcast(FP8X4), rhs_scale=z_plane[:], start=False, stop=last_piece,
                 )
 
         ea = sb.tile([P, PACK, S], F32, name="ea")
@@ -240,32 +254,22 @@ def tile_picked_pqmixemoera_none_po_kernel(
         out_rows = out_0.rearrange("(p t) j -> p t j", t=PACK)
         out_words = words_of(out_1)
         y_plane = sb.tile([P, S], U8, name="y_plane", align_bytes=64)
-        width = 128
-        count = S // width
-        cols = [slice(c * width, (c + 1) * width) for c in range(count)]
-        slot = PACK * width * 4
-        roots, factors, ys, y_bfs = [], [], [], []
-        for c in range(count + 1):
-            if c < count:
-                roots.append(tail.tile([P, PACK, width], F32, name=f"root{c}", align_bytes=64, offset=c * slot))
-                nc.scalar.activation(roots[c][:], ea[:, :, cols[c]], ACT.Abs_reciprocal_sqrt, bias=0.5, scale=2.0)
-            if c > 0:
-                factors.append(sb.tile([P, PACK, width], F32, name=f"factor{c - 1}"))
-                nc.scalar.activation(factors[c - 1][:], roots[c - 1][:], ACT.Square)
-        for c in range(count + 2):
-            if c < count:
-                ys.append(sb.tile([P, PACK, width], F32, name=f"y{c}"))
-                nc.vector.tensor_tensor(ys[c][:], diff[:, :, cols[c]], factors[c][:], ALU.mult)
-                nc.sync.dma_start(out_rows[:, :, cols[c]], ys[c][:])
-            if 1 <= c <= count:
-                y_bfs.append(tail.tile([P, width, PACK], BF16, name=f"y_bf{c - 1}", align_bytes=64, offset=c * slot))
-                nc.vector.tensor_copy(y_bfs[c - 1][:], ys[c - 1][:].rearrange("p t j -> p j t"))
-            if c >= 2:
-                y_codes = tail.tile([P, width], U32, name=f"y_codes{c - 2}", align_bytes=64, offset=c * slot + slot // 2)
-                nc.vector.quantize_mx(
-                    out=y_codes[:].bitcast(FP8X4), scales=y_plane[:, cols[c - 2]], in_=y_bfs[c - 2][:].rearrange("p j t -> p (j t)")
-                )
-                nc.sync.dma_start(out_words[:, cols[c - 2]], y_codes[:].bitcast(I32))
-        for q in range(4):
+        for piece, start in enumerate(range(0, S, OUT_WIDTH)):
+            cols = slice(start, start + OUT_WIDTH)
+            root = sb.tile([P, PACK, OUT_WIDTH], F32, name=f"root{piece}")
+            nc.scalar.activation(root[:], ea[:, :, cols], ACT.Abs_reciprocal_sqrt, bias=0.5, scale=2.0)
+            factor = sb.tile([P, PACK, OUT_WIDTH], F32, name=f"factor{piece}")
+            nc.scalar.activation(factor[:], root[:], ACT.Square)
+            y = sb.tile([P, PACK, OUT_WIDTH], F32, name=f"y{piece}")
+            nc.vector.tensor_tensor(y[:], diff[:, :, cols], factor[:], ALU.mult)
+            nc.sync.dma_start(out_rows[:, :, cols], y[:])
+            y_bf = sb.tile([P, OUT_WIDTH, PACK], BF16, name=f"y_bf{piece}", align_bytes=64)
+            nc.vector.tensor_copy(
+                y_bf[:].rearrange("p (c i) t -> p c t i", i=WORD_RUN), y[:].rearrange("p t (c i) -> p c t i", i=WORD_RUN)
+            )
+            y_codes = sb.tile([P, OUT_WIDTH], U32, name=f"y_codes{piece}", align_bytes=64)
+            nc.vector.quantize_mx(out=y_codes[:].bitcast(FP8X4), scales=y_plane[:, cols], in_=y_bf[:].rearrange("p j t -> p (j t)"))
+            nc.sync.dma_start(out_words[:, cols], y_codes[:].bitcast(I32))
+        for q in range(QUADRANTS):
             queue = nc.scalar if q % 2 else nc.sync
             queue.dma_start(out_2[0, 4 * q : 4 * q + 4, :].bitcast(I32), y_plane[32 * q : 32 * q + 4, :].bitcast(I32))

from contextlib import ExitStack

import concourse.mybir as mybir

F32 = mybir.dt.float32
BF16 = mybir.dt.bfloat16
I32 = mybir.dt.int32
U32 = mybir.dt.uint32
U16 = mybir.dt.uint16
U8 = mybir.dt.uint8
FP8X4 = mybir.dt.float8_e4m3fn_x4
ALU = mybir.AluOpType
ACT = mybir.ActivationFunctionType

P = 128
PACK = 4
QUADRANTS = 4
T, G = 1024, 2048
S = 512
N = 512
FLOPS = 3 * 2 * 512 * 512 * 512

WORD_RUN, BYTE_RUN = 4, 16
W2_PLANE = 4

HALVES = ((0, 256), (256, 256))
Z_PIECES = ((0, 256), (256, 128), (384, 128))
MAX_RUNS = (((0, 1), (1, 2), (2, 3), (3, 4)), ((0, 4),), ((0, 3), (3, 4)))
OUT_WIDTH = 128

X2_CODES_AT, X2_PLANE_AT = 0, 2048
DK_FIRST_AT = X2_PLANE_AT - 256
D_TABLE_AT = 8192


def words_of(dram):
    return dram[0].rearrange("p n r -> p (n r)").bitcast(I32)


def entries(offsets, start, width):
    return offsets[:, start // 16 : (start + width) // 16]


def deal(copy, dst, src, run):
    copy(
        out=dst.rearrange("p (t c i) -> p c t i", t=PACK, i=run),
        in_=src.rearrange("p (c i t) -> p c t i", t=PACK, i=run),
    )


def tile_picked_pqmixemoera_none_po_kernel(
    tc, x_words, x_scales, d_words, d_scales, sl, th, gn, w1_words, w1_scales, w2_words, w2_scales, tau,
    offs, k1, n1, n2, two, n3, n4, out_0, out_1, out_2,
):
    nc = tc.nc
    with ExitStack() as ctx:
        lists = ctx.enter_context(tc.tile_pool(name="lists", bufs=1))
        sb = ctx.enter_context(tc.tile_pool(name="sb", bufs=1))
        shared = ctx.enter_context(tc.tile_pool(name="shared", bufs=1))
        psum = ctx.enter_context(tc.psum_pool(name="psum", bufs=1))

        def load_list(dram, name):
            offsets = lists.tile([P, S // 16], U16, name=name)
            nc.sync.dma_start(offsets[:], dram)
            return offsets

        def load_rows(dram, name):
            values = sb.tile([P, PACK], F32, name=name)
            nc.gpsimd.dma_start(values[:], dram.rearrange("(p t) o -> p (t o)", t=PACK))
            return values

        warm_in = sb.tile([P, 1], F32, name="warm_in")
        nc.vector.memset(warm_in[:], 0.0)
        warm_sigmoid = sb.tile([P, 1], F32, name="warm_sigmoid")
        nc.scalar.activation(warm_sigmoid[:], warm_in[:], ACT.Sigmoid)

        h2_rows = [sb.tile([P, 2 * S], F32, name=f"h2_rows{t}") for t in range(PACK)]

        k1_sb = load_list(k1, "k1_sb")
        d_bytes = sb.tile([P, G], U8, name="d_bytes")
        nc.sync.dma_start(
            d_bytes[:].bitcast(I32),
            d_scales[0].bitcast(I32).unsqueeze(1).to_broadcast([16, 8, G // 4]),
        )
        offs_sb = load_list(offs, "offs_sb")
        x_bytes = sb.tile([P, T], U8, name="x_bytes")
        for q in range(QUADRANTS):
            (nc.scalar if q < QUADRANTS - 1 else nc.sync).dma_start(
                x_bytes[32 * q : 32 * q + 32, :].bitcast(I32),
                x_scales[0, 4 * q : 4 * q + 4, :].bitcast(I32).unsqueeze(0).to_broadcast([8, 4, T // 4]),
            )
        d_table = shared.tile([P, G], I32, name="d_table", align_bytes=64, offset=D_TABLE_AT)
        nc.sync.dma_start(d_table[:], words_of(d_words))
        x_table = sb.tile([P, T], I32, name="x_table")
        nc.sync.dma_start(x_table[:], words_of(x_words))
        w2_raw = sb.tile([P, N], I32, name="w2_raw")
        nc.sync.dma_start(w2_raw[:], words_of(w2_words))
        w1_raw = sb.tile([P, N], I32, name="w1_raw")
        nc.sync.dma_start(w1_raw[:], words_of(w1_words))
        n1_sb = load_list(n1, "n1_sb")
        n2_sb = load_list(n2, "n2_sb")
        two_sb = load_list(two, "two_sb")
        sl_sb = load_rows(sl, "sl_sb")
        th_sb = load_rows(th, "th_sb")
        sl_th = sb.tile([P, PACK], F32, name="sl_th")
        nc.gpsimd.tensor_tensor(sl_th[:], sl_sb[:], th_sb[:], ALU.mult)
        sg_bias = sb.tile([P, PACK], F32, name="sg_bias")
        nc.gpsimd.tensor_scalar(sg_bias[:], sl_th[:], -1.0, 1.0, ALU.mult, ALU.mult)
        gn_sb = load_rows(gn, "gn_sb")
        tau_sb = load_rows(tau, "tau_sb")

        dk_bytes = sb.tile([P, S], U8, name="dk_bytes", tag="w_bytes")
        nc.vector.tensor_copy(dk_bytes[:], d_bytes[:].indirect(k1_sb[:]))
        dk_plane = sb.tile([P, S], U8, name="dk_plane", align_bytes=64)
        deal(nc.vector.tensor_copy, dk_plane[:], dk_bytes[:], BYTE_RUN)
        for a in range(1, 4):
            nc.scalar.dma_start(dk_plane[a:P:32, :].bitcast(I32), dk_plane[8 * a : P : 32, :].bitcast(I32))
        w_bytes = sb.tile([P, N], U8, name="w_bytes", tag="w_bytes")
        nc.gpsimd.memset(w_bytes[:].bitcast(I32), 0)
        for place, scales, queue in ((W2_PLANE, w2_scales, nc.sync), (0, w1_scales, nc.gpsimd)):
            for q in range(QUADRANTS):
                queue.dma_start(
                    w_bytes[32 * q + place : 32 * q + place + 4, :].bitcast(I32),
                    scales[0, 4 * q : 4 * q + 4, :].bitcast(I32),
                )
        n4_sb = load_list(n4, "n4_sb")
        n3_sb = load_list(n3, "n3_sb")
        xq_plane = sb.tile([P, S], U8, name="xq_plane", align_bytes=64)
        nc.vector.tensor_copy(xq_plane[:], x_bytes[:].indirect(offs_sb[:]))
        dk_words = sb.tile([P, S], U32, name="dk_words")
        nc.vector.tensor_copy(dk_words[:], d_table[:].bitcast(U32).indirect(k1_sb[:]))
        dk_first = shared.tile([P, P], I32, name="dk_first", align_bytes=64, offset=DK_FIRST_AT)
        dk_rest = sb.tile([P, PACK - 1, P], I32, name="dk_rest", tag="w_planes", align_bytes=64)
        dk_codes = [dk_first[:]] + [dk_rest[:, t, :] for t in range(PACK - 1)]
        nc.vector.tensor_copy(dk_first[:], dk_words[:].bitcast(I32)[:, 0::PACK])
        xq_codes = shared.tile([P, S], U32, name="xq_codes", align_bytes=64, offset=D_TABLE_AT)
        for start, width in HALVES:
            nc.vector.tensor_copy(
                xq_codes[:, start : start + width], x_table[:].bitcast(U32).indirect(entries(offs_sb, start, width))
            )

        w2_codes = sb.tile([P, N], U32, name="w2_codes", align_bytes=64)
        deal(nc.scalar.copy, w2_codes[:], w2_raw[:].bitcast(U32), WORD_RUN)
        w1_codes = sb.tile([P, N], U32, name="w1_codes", align_bytes=64)
        deal(nc.scalar.copy, w1_codes[:], w1_raw[:].bitcast(U32), WORD_RUN)

        h_rows = [sb.tile([P, S], F32, name=f"h_rows{t}") for t in range(PACK)]

        def first_product(t, start, width, bank_name):
            bank = psum.tile([P, S], F32, name=bank_name, bufs=3 if bank_name == "h_bank" else 1)
            rows, cols = slice(P * t, P * (t + 1)), slice(start, start + width)
            nc.tensor.matmul_mx(
                out=bank[:, :width], lhsT=dk_codes[t].bitcast(FP8X4), lhsT_scale=dk_plane[:, rows],
                rhs=xq_codes[:, cols].bitcast(FP8X4), rhs_scale=xq_plane[:, cols], start=True, stop=True,
            )
            return bank[:, :width]

        for (start, width), bank_name in zip(HALVES, ("h_first", "h_bank")):
            nc.scalar.activation(
                h_rows[0][:, start : start + width], first_product(0, start, width, bank_name), ACT.Copy, scale=0.0625
            )
        nc.vector.tensor_copy(
            dk_rest[:].rearrange("p t (c i) -> p c t i", i=WORD_RUN),
            dk_words[:].bitcast(I32).rearrange("p (c i t) -> p c t i", t=PACK, i=WORD_RUN)[:, :, 1:, :],
        )

        nc.scalar.activation(h_rows[1][:], first_product(1, 0, S, "h_bank"), ACT.Copy, scale=0.0625)
        for t in range(2, PACK):
            nc.vector.tensor_scalar(h_rows[t][:], first_product(t, 0, S, "h_bank"), 0.0625, None, ALU.mult)

        x2_codes = shared.tile([P, S], U32, name="x2_codes", align_bytes=64, offset=X2_CODES_AT)
        nc.vector.tensor_copy(x2_codes[:], x_table[:].bitcast(U32).indirect(two_sb[:]))
        x2_plane = shared.tile([P, S], U8, name="x2_plane", align_bytes=64, offset=X2_PLANE_AT)
        nc.vector.tensor_copy(x2_plane[:], x_bytes[:].indirect(two_sb[:]))

        h2_banks = [psum.tile([P, S], F32, name=f"h2_bank{t}") for t in range(PACK)]
        w_planes = sb.tile([P, N], U8, name="w_planes", tag="w_planes", align_bytes=64)
        deal(nc.vector.tensor_copy, w_planes[:], w_bytes[:], BYTE_RUN)
        for t in range(PACK):
            rows = slice(P * t, P * (t + 1))
            nc.tensor.matmul_mx(
                out=h2_banks[t][:], lhsT=w2_codes[:, rows].bitcast(FP8X4), lhsT_scale=w_planes[W2_PLANE:P, rows],
                rhs=x2_codes[:].bitcast(FP8X4), rhs_scale=x2_plane[:], start=True, stop=False,
            )

        for piece, (start, width) in enumerate(Z_PIECES):
            cols = slice(start, start + width)
            last_piece = start + width == S
            sg = [h2_rows[t][:, S + start : S + start + width] for t in range(PACK)]
            h_n2 = sb.tile([P, PACK, width], F32, name=f"h_n2{piece}")
            gated = sb.tile([P, PACK, width], F32, name=f"gated{piece}")
            larger = sb.tile([P, PACK, width], F32, name=f"larger{piece}")
            for first, end in MAX_RUNS[piece]:
                for t in range(first, end):
                    nc.scalar.activation(
                        sg[t], h_rows[t][:].indirect(entries(n1_sb, start, width)), ACT.Sigmoid,
                        bias=sg_bias[:, t : t + 1], scale=sl_sb[:, t : t + 1],
                    )
                    nc.scalar.activation(h_n2[:, t, :], h_rows[t][:].indirect(entries(n2_sb, start, width)), ACT.Copy)
                    nc.vector.tensor_tensor(gated[:, t, :], h_rows[t][:, cols], sg[t], ALU.mult)
                nc.vector.scalar_tensor_tensor(
                    larger[:, first:end, :], h_n2[:, first:end, :], 0.75, gated[:, first:end, :], ALU.mult, ALU.max
                )
            if last_piece:
                warm_exp = sb.tile([P, 1], F32, name="warm_exp")
                nc.scalar.activation(warm_exp[:], sg[PACK - 1][:, :1], ACT.Exp)
            z = sb.tile([P, width, PACK], BF16, name=f"z{piece}", align_bytes=64)
            nc.vector.tensor_tensor(
                z[:].rearrange("p (c i) t -> p c t i", i=WORD_RUN),
                larger[:].rearrange("p t (c i) -> p c t i", i=WORD_RUN),
                gn_sb[:].unsqueeze(1).unsqueeze(3).to_broadcast([P, width // WORD_RUN, PACK, WORD_RUN]),
                ALU.mult,
            )
            z_codes = sb.tile([P, width], U32, name=f"z_codes{piece}", align_bytes=64)
            z_plane = sb.tile([P, width], U8, name=f"z_plane{piece}", align_bytes=64)
            nc.vector.quantize_mx(out=z_codes[:].bitcast(FP8X4), scales=z_plane[:], in_=z[:].rearrange("p j t -> p (j t)"))
            for t in range(PACK):
                rows = slice(P * t, P * (t + 1))
                nc.tensor.matmul_mx(
                    out=h2_banks[t][:, cols], lhsT=w1_codes[:, rows].bitcast(FP8X4), lhsT_scale=w_planes[:, rows],
                    rhs=z_codes[:].bitcast(FP8X4), rhs_scale=z_plane[:], start=False, stop=last_piece,
                )

        ea = sb.tile([P, PACK, S], F32, name="ea")
        top = sb.tile([P, PACK], F32, name="top")
        ea_bias = sb.tile([P, PACK], F32, name="ea_bias")
        h2_n3 = sb.tile([P, PACK, S], F32, name="h2_n3")
        diff = sb.tile([P, PACK, S], F32, name="diff")

        def leave_bank(t):
            nc.vector.tensor_scalar(
                h2_rows[t][:, :S], h2_banks[t][:], 1.0, None, ALU.mult, ALU.max, accum_out=top[:, t : t + 1]
            )

        def exponential(t):
            nc.gpsimd.tensor_scalar(ea_bias[:, t : t + 1], top[:, t : t + 1], tau_sb[:, t : t + 1], -1.0, ALU.mult, ALU.mult)
            nc.scalar.activation(
                ea[:, t, :], h2_rows[t][:].indirect(n4_sb[:]), ACT.Exp, bias=ea_bias[:, t : t + 1], scale=tau_sb[:, t : t + 1]
            )

        leave_bank(0)
        exponential(0)
        leave_bank(1)
        for t in range(1, PACK):
            if t + 1 < PACK:
                leave_bank(t + 1)
            exponential(t)
        for t in range(PACK + 1):
            if t < PACK:
                nc.vector.tensor_copy(h2_n3[:, t, :], h2_rows[t][:].indirect(n3_sb[:]))
            if t > 0:
                nc.vector.tensor_tensor(diff[:, t - 1, :], h2_banks[t - 1][:], h2_n3[:, t - 1, :], ALU.subtract)

        out_rows = out_0.rearrange("(p t) j -> p t j", t=PACK)
        out_words = words_of(out_1)
        y_plane = sb.tile([P, S], U8, name="y_plane", align_bytes=64)
        for piece, start in enumerate(range(0, S, OUT_WIDTH)):
            cols = slice(start, start + OUT_WIDTH)
            root = sb.tile([P, PACK, OUT_WIDTH], F32, name=f"root{piece}")
            nc.scalar.activation(root[:], ea[:, :, cols], ACT.Abs_reciprocal_sqrt, bias=0.5, scale=2.0)
            factor = sb.tile([P, PACK, OUT_WIDTH], F32, name=f"factor{piece}")
            nc.scalar.activation(factor[:], root[:], ACT.Square)
            y = sb.tile([P, PACK, OUT_WIDTH], F32, name=f"y{piece}")
            nc.vector.tensor_tensor(y[:], diff[:, :, cols], factor[:], ALU.mult)
            nc.sync.dma_start(out_rows[:, :, cols], y[:])
            y_bf = sb.tile([P, OUT_WIDTH, PACK], BF16, name=f"y_bf{piece}", align_bytes=64)
            nc.vector.tensor_copy(
                y_bf[:].rearrange("p (c i) t -> p c t i", i=WORD_RUN), y[:].rearrange("p t (c i) -> p c t i", i=WORD_RUN)
            )
            y_codes = sb.tile([P, OUT_WIDTH], U32, name=f"y_codes{piece}", align_bytes=64)
            nc.vector.quantize_mx(out=y_codes[:].bitcast(FP8X4), scales=y_plane[:, cols], in_=y_bf[:].rearrange("p j t -> p (j t)"))
            nc.sync.dma_start(out_words[:, cols], y_codes[:].bitcast(I32))
        for q in range(QUADRANTS):
            queue = nc.scalar if q % 2 else nc.sync
            queue.dma_start(out_2[0, 4 * q : 4 * q + 4, :].bitcast(I32), y_plane[32 * q : 32 * q + 4, :].bitcast(I32))
